import numpy as np
import ml_dtypes


def mxq(x, axis, fmt="e4m3"):
    dtype, down = {"e4m3": (ml_dtypes.float8_e4m3fn, 7), "e5m2": (ml_dtypes.float8_e5m2, 14)}[fmt]
    v = np.moveaxis(np.asarray(x, np.float32).astype(ml_dtypes.bfloat16).astype(np.float64), axis, -1)
    blocks = v.reshape(v.shape[:-1] + (-1, 32))
    amax = np.abs(blocks).max(-1, keepdims=True)
    byte = np.maximum(np.where(amax > 0, np.frexp(amax)[1] - 1 + 127, 0) - down, 1)
    scale = np.exp2(byte - 127.0)
    codes = (blocks / scale).astype(np.float32).astype(dtype).astype(np.float64)
    return np.moveaxis((codes * scale).reshape(v.shape), -1, axis)


WIDE = False


def mx_kscale(k):
    if not WIDE:
        return np.ones(k)
    levels = np.array([10, -10, 5, -5, 0])
    if k % 512:
        return np.exp2(np.random.permutation(np.resize(levels, k // 32))).repeat(32)
    a = np.empty((k // 512, 16))
    for p in range(k // 512):
        a[p, :8] = np.random.permutation(np.resize(levels, 8))
        for g in range(8):
            far = levels[np.abs(levels - a[p, g]) >= 10]
            a[p, g + 8] = far[np.random.randint(len(far))]
    return np.exp2(a.ravel()).repeat(32)


def f64(x):
    return np.asarray(x).astype(np.float64)


def striped8(idx):
    return np.asarray(idx).reshape(8, -1, 16).transpose(0, 2, 1).reshape(128, -1).astype(np.uint16)


def unstriped8(offs):
    return offs.reshape(8, 16, -1).transpose(0, 2, 1).reshape(8, -1).astype(np.int64)


def pick8(x, idx, run):
    r = np.arange(len(x))
    return x[r[:, None], idx[r % (8 * run) // run]]


E2M1 = np.array([0.0, 0.5, 1.0, 1.5, 2.0, 3.0, 4.0, 6.0, -0.0, -0.5, -1.0, -1.5, -2.0, -3.0, -4.0, -6.0])


def pack_weight(w, fmt):
    k, n = w.shape
    w = f64(np.asarray(w, np.float32).astype(ml_dtypes.bfloat16)).reshape(k // 32, 32, n)
    amax = np.abs(w).max(1)
    if fmt == "e4m3":
        byte = np.frexp(amax)[1] - 1 + 127 - 7
    else:
        mant, ex = np.frexp(amax / 6.0)
        byte = np.where(mant > 0.5, ex, ex - 1) + 127
    byte = np.clip(np.where(amax > 0, byte, 1), 1, 254)
    scaled = (w * np.exp2(127.0 - byte)[:, None, :]).reshape(k, n).astype(np.float32)
    by_word = np.ascontiguousarray(scaled.reshape(k // 512, 128, 4, n).transpose(0, 1, 3, 2))
    if fmt == "e4m3":
        words = by_word.astype(ml_dtypes.float8_e4m3fn).view(np.uint8)
    else:
        c = by_word.astype(ml_dtypes.float4_e2m1fn).view(np.uint8) & 0xF
        words = (c[..., 0::2] | (c[..., 1::2] << 4)).reshape(k // 512, 128, 2 * n)
    return np.ascontiguousarray(words), np.ascontiguousarray(byte.astype(np.uint8).reshape(k // 512, 16, n))


def unpack_weight(words, scales, fmt):
    g, _, n = scales.shape
    words = np.ascontiguousarray(words).reshape(g, 128, n, -1)
    if fmt == "e4m3":
        vals = words.view(ml_dtypes.float8_e4m3fn).astype(np.float64)
    else:
        nib = np.empty((g, 128, n, 4), np.uint8)
        nib[..., 0::2] = words & 0xF
        nib[..., 1::2] = words >> 4
        vals = E2M1[nib]
    vals = vals * np.repeat(np.exp2(scales.astype(np.float64) - 127.0), 8, axis=1)[..., None]
    return vals.transpose(0, 1, 3, 2).reshape(g * 512, n)


def sigmoid(v):
    return 1.0 / (1.0 + np.exp(-v))


D, T, U, X, I, J, Q, E = 512, 1024, 1024, 1024, 512, 256, 512, 256


def setup_inputs():
    n = np.random.standard_normal
    idx = np.stack([np.random.permutation(T)[:I] for _ in range(8)])
    idx2 = np.stack([np.random.permutation(U)[:I] for _ in range(8)])
    idx3 = np.stack([np.random.permutation(X)[:J] for _ in range(8)])
    idx4 = np.stack([np.random.permutation(X)[:I] for _ in range(8)])
    fd = mx_kscale(D)
    fq = mx_kscale(Q)
    keysp = pack_weight(n((D, T)) / fd[:, None], "e2m1")
    notesp = pack_weight(n((D, U)) / fd[:, None], "e4m3")
    usersp = pack_weight(n((D, X)) / fd[:, None], "e4m3")
    mixp = pack_weight(n((Q, E)) * 1.0 / np.sqrt(Q) / fq[:, None], "e4m3")
    return {
        "query": (n((D, Q)) * 1.0 / np.sqrt(D) * fd[:, None]).astype(np.float32),
        "query2": (n((D, Q)) * 1.0 / np.sqrt(D) * fd[:, None]).astype(np.float32),
        "keys_words": keysp[0],
        "keys_scales": keysp[1],
        "notes_words": notesp[0],
        "notes_scales": notesp[1],
        "users_words": usersp[0],
        "users_scales": usersp[1],
        "thr": (np.random.uniform(-0.6, 0.6, (Q, 1))).astype(np.float32),
        "slope": (np.random.uniform(1.0, 3.0, (Q, 1))).astype(np.float32),
        "rowf": (np.random.uniform(0.5, 2.0, (Q, 1)) * fq[:, None]).astype(np.float32),
        "mix_words": mixp[0],
        "mix_scales": mixp[1],
        "offs": striped8(idx),
        "offs2": striped8(idx2),
        "offs3": striped8(idx3),
        "offs4": striped8(idx4),
    }


def reference(query, query2, keys_words, keys_scales, notes_words, notes_scales, users_words, users_scales, thr, slope, rowf, mix_words, mix_scales, offs, offs2, offs3, offs4):
    idx = unstriped8(offs)
    idx2 = unstriped8(offs2)
    idx3 = unstriped8(offs3)
    idx4 = unstriped8(offs4)
    keysu = unpack_weight(keys_words, keys_scales, "e2m1")
    notesu = unpack_weight(notes_words, notes_scales, "e4m3")
    usersu = unpack_weight(users_words, users_scales, "e4m3")
    mixu = unpack_weight(mix_words, mix_scales, "e4m3")
    queryq = mxq(f64(query), 0, "e4m3")
    a = queryq.T @ keysu
    b = queryq.T @ notesu
    query2q = mxq(f64(query2), 0, "e4m3")
    c0 = query2q.T @ usersu
    s1 = sigmoid(pick8(a, idx, 64) * f64(slope) + f64(thr))
    w = pick8(b, idx2, 64) * s1
    p2 = w.reshape(Q, J, I // J).sum(axis=2)
    f1 = np.zeros((Q, X))
    f1[np.arange(Q)[:, None], idx3[np.arange(Q) % 512 // 64]] = p2
    cc = c0 + f1
    g = pick8(cc, idx4, 64)
    gw = g * f64(rowf)
    gwq = mxq(gw, 0, "e4m3")
    y = mixu.T @ gwq
    return y

@@ -1,0 +1,210 @@
+from contextlib import ExitStack
+
+import concourse.mybir as mybir
+
+F32 = mybir.dt.float32
+BF16 = mybir.dt.bfloat16
+I32 = mybir.dt.int32
+U32 = mybir.dt.uint32
+U16 = mybir.dt.uint16
+U8 = mybir.dt.uint8
+FP8X4 = mybir.dt.float8_e4m3fn_x4
+FP4X4 = mybir.dt.float4_e2m1fn_x4
+ACT = mybir.ActivationFunctionType
+ALU = mybir.AluOpType
+
+P = 128
+PACK = 4
+D, T, I, J, Q, E = 512, 1024, 512, 256, 512, 256
+BANK = 512
+FLOPS = 2 * D * Q * 3 * T + 2 * Q * E * I
+
+
+def tile_attend_pairopen_threeq_mixed_kernel(tc, query, query2, keys_words, keys_scales, notes_words, notes_scales,
+                                              users_words, users_scales, thr, slope, rowf, mix_words, mix_scales,
+                                              offs, offs2, offs3, offs4, out):
+    nc = tc.nc
+    with ExitStack() as ctx:
+        keep = ctx.enter_context(tc.tile_pool(name="keep", bufs=1))
+        ring = ctx.enter_context(tc.tile_pool(name="ring", bufs=2))
+        psum = ctx.enter_context(tc.psum_pool(name="psum", bufs=1))
+
+        def plane(name, width, engine):
+            t = keep.tile([P, width], U8, name=name, align_bytes=64)
+            engine.memset(t[:].bitcast(I32), 0)
+            return t
+
+        def load_plane(queue, t, src):
+            for quad in range(4):
+                queue.dma_start(out=t[32 * quad:32 * quad + 4, :].bitcast(I32),
+                                in_=src[0, 4 * quad:4 * quad + 4, :].bitcast(I32))
+
+        def load_words(t, src):
+            nc.sync.dma_start(out=t[:].bitcast(I32), in_=src[0].rearrange("p n t -> p (n t)").bitcast(I32))
+
+        def load_query(name, src, h, tag=None):
+            t = keep.tile([P, PACK, Q // 2], F32, name="%s%d" % (name, h), tag=tag or "%s%d" % (name, h), align_bytes=64)
+            nc.sync.dma_start(out=t[:], in_=src.rearrange("(p t) q -> p t q", t=PACK)[:, :, h * 256:(h + 1) * 256])
+            return t
+
+        def load_list(name, src, n):
+            t = keep.tile([P, n // 16], U16, name=name)
+            nc.sync.dma_start(t[:], src)
+            return t
+
+        def load_rows(name, src):
+            t = keep.tile([P, PACK], F32, name=name)
+            nc.sync.dma_start(out=t[:], in_=src.rearrange("(p r) o -> p (r o)", r=PACK))
+            return t
+
+        keys_sc = plane("keys_sc", T, nc.gpsimd)
+        notes_sc = plane("notes_sc", T, nc.gpsimd)
+        users_sc = plane("users_sc", T, nc.vector)
+        mix_sc = plane("mix_sc", E, nc.vector)
+        f1 = keep.tile([P, T], F32, name="f1")
+        nc.vector.memset(f1[:], 0.0)
+
+        keys_w = keep.tile([P, 2 * T], U8, name="keys_w", align_bytes=64)
+        notes_w = keep.tile([P, T], U32, name="notes_w", align_bytes=64)
+        users_w = keep.tile([P, T], U32, name="users_w", align_bytes=64)
+        mix_w = keep.tile([P, E], U32, name="mix_w", align_bytes=64)
+
+        q1_raw = [load_query("q1_raw", query, 0)]
+        load_plane(nc.sync, keys_sc, keys_scales)
+        q1_raw.append(load_query("q1_raw", query, 1))
+        nc.sync.dma_start(out=keys_w[:].bitcast(I32), in_=keys_words[0].bitcast(I32))
+        load_words(notes_w, notes_words)
+        list_a = load_list("list_a", offs, I)
+        slope_t = load_rows("slope_t", slope)
+        thr_t = load_rows("thr_t", thr)
+        load_plane(nc.sync, notes_sc, notes_scales)
+        q2_raw = [load_query("q2_raw", query2, 0)]
+        list_b = load_list("list_b", offs2, I)
+        q2_raw.append(load_query("q2_raw", query2, 1, "shared"))
+        load_plane(nc.sync, users_sc, users_scales)
+        load_words(users_w, users_words)
+        list_p = load_list("list_p", offs3, J)
+        list_g = load_list("list_g", offs4, I)
+        rowf_t = load_rows("rowf_t", rowf)
+        load_words(mix_w, mix_words)
+        load_plane(nc.sync, mix_sc, mix_scales)
+
+        def deal(copy, dealt, raw, h):
+            copy(out=dealt[:, :, 64 * h:64 * h + 64, :].rearrange("p r m t -> p m r t"),
+                 in_=raw[:].rearrange("p t (m r) -> p m r t", r=PACK))
+
+        def quantise(codes, scales, dealt, r0, r1):
+            nc.vector.quantize_mx(out=codes[:, r0 * P:r1 * P].bitcast(FP8X4), scales=scales[:, r0 * P:r1 * P],
+                                  in_=dealt[:, r0:r1, :, :].rearrange("p r m t -> p (r m t)"))
+
+        q1_bf = keep.tile([P, PACK, P, PACK], BF16, name="q1_bf", align_bytes=64)
+        q1_w = keep.tile([P, Q], U32, name="q1_w", align_bytes=64)
+        q2_w = keep.tile([P, Q], U32, name="q2_w", align_bytes=64)
+        q1_sc = keep.tile([P, Q], U8, name="q1_sc", align_bytes=64)
+        q2_sc = keep.tile([P, Q], U8, name="q2_sc", align_bytes=64)
+
+        def scores(tag, q_w, q_sc, rhs_of, rhs_sc, r):
+            banks = []
+            for h in range(2):
+                bank = psum.tile([P, BANK], F32, name="%s%d" % (tag, h))
+                nc.tensor.matmul_mx(out=bank[:], lhsT=q_w[:, r * P:(r + 1) * P].bitcast(FP8X4),
+                                    lhsT_scale=q_sc[:, r * P:(r + 1) * P], rhs=rhs_of(h),
+                                    rhs_scale=rhs_sc[:, h * BANK:(h + 1) * BANK], start=True, stop=True)
+                banks.append(bank)
+            return banks
+
+        def keys_rhs(h):
+            return keys_w[:, 2 * h * BANK:2 * (h + 1) * BANK].bitcast(FP4X4)
+
+        def notes_rhs(h):
+            return notes_w[:, h * BANK:(h + 1) * BANK].bitcast(FP8X4)
+
+        def users_rhs(h):
+            return users_w[:, h * BANK:(h + 1) * BANK].bitcast(FP8X4)
+
+        def to_sbuf(t, banks, copy):
+            for h in range(2):
+                copy(out=t[:, h * BANK:(h + 1) * BANK], in_=banks[h][:])
+            return t
+
+        def gate(a_sb, r):
+            s1 = ring.tile([P, I], F32, name="s1")
+            nc.scalar.activation(out=s1[:], in_=a_sb[:].indirect(list_a[:]), func=ACT.Sigmoid,
+                                 bias=thr_t[:, r:r + 1], scale=slope_t[:, r:r + 1])
+            return s1
+
+        def front(r, copy):
+            a_banks = scores("a", q1_w, q1_sc, keys_rhs, keys_sc, r)
+            b_banks = scores("b", q1_w, q1_sc, notes_rhs, notes_sc, r)
+            a_sb = to_sbuf(keep.tile([P, T], F32, name="a_sb", tag="a_first" if r == 0 else "shared", align_bytes=64), a_banks, copy)
+            b_sb = to_sbuf(ring.tile([P, T], F32, name="b_sb"), b_banks, copy)
+            return gate(a_sb, r), b_sb
+
+        def pairs(s1, b_sb):
+            w = ring.tile([P, I], F32, name="w")
+            nc.vector.tensor_tensor(out=w[:], in0=b_sb[:].indirect(list_b[:]), in1=s1[:], op=ALU.mult)
+            p2 = ring.tile([P, J], F32, name="p2")
+            nc.vector.tensor_tensor(out=p2[:], in0=w[:, 0:I:2], in1=w[:, 1:I:2], op=ALU.add)
+            nc.vector.tensor_copy(out=f1[:].indirect(list_p[:]), in_=p2[:])
+
+        def users_sum(r):
+            c_banks = scores("c", q2_w, q2_sc, users_rhs, users_sc, r)
+            cc = keep.tile([P, T], F32, name="cc%d" % r)
+            for h in range(2):
+                cols = slice(h * BANK, (h + 1) * BANK)
+                nc.vector.tensor_tensor(out=cc[:, cols], in0=c_banks[h][:], in1=f1[:, cols], op=ALU.add)
+            return cc
+
+        gw3 = keep.tile([P, PACK - 1, I], F32, name="gw3")
+        gw_bf = keep.tile([P, I, PACK], BF16, name="gw_bf", align_bytes=64)
+
+        deal(nc.scalar.copy, q1_bf, q1_raw[0], 0)
+        deal(nc.vector.tensor_copy, q1_bf, q1_raw[1], 1)
+        quantise(q1_w, q1_sc, q1_bf, 0, 1)
+        quantise(q1_w, q1_sc, q1_bf, 1, 4)
+
+        ready = front(0, nc.vector.tensor_copy)
+        q2_bf = keep.tile([P, PACK, P, PACK], BF16, name="q2_bf", tag="a_first", align_bytes=64)
+        deal(nc.scalar.copy, q2_bf, q2_raw[0], 0)
+        deal(nc.scalar.copy, q2_bf, q2_raw[1], 1)
+        sums = []
+        for r in range(PACK):
+            s1, b_sb = ready
+            if r + 1 < PACK:
+                ready = front(r + 1, nc.scalar.copy)
+            pairs(s1, b_sb)
+            if r == 0:
+                quantise(q2_w, q2_sc, q2_bf, 0, 4)
+            sums.append(users_sum(r))
+        for r in range(PACK - 1):
+            g = ring.tile([P, I], F32, name="g")
+            nc.scalar.activation(out=g[:], in_=sums[r][:].indirect(list_g[:]), func=ACT.Copy)
+            nc.scalar.activation(out=gw3[:, r, :], in_=g[:], func=ACT.Copy, scale=rowf_t[:, r:r + 1])
+        nc.vector.tensor_copy(out=gw_bf[:, :, 0:3], in_=gw3[:].rearrange("p r i -> p i r"))
+        cc = sums[PACK - 1]
+
+        half = I // 2
+        g_last = [keep.tile([P, half], F32, name="g_last%d" % h) for h in range(2)]
+        nc.vector.tensor_copy(out=g_last[0][:], in_=cc[:].indirect(list_g[:, 0:16]))
+        nc.scalar.activation(out=g_last[1][:], in_=cc[:].indirect(list_g[:, 16:32]), func=ACT.Copy)
+        gw_w = keep.tile([P, I], U32, name="gw_w", align_bytes=64)
+        gw_sc = keep.tile([P, I], U8, name="gw_sc", align_bytes=64)
+        for h in range(2):
+            cols = slice(h * half, (h + 1) * half)
+            nc.vector.tensor_scalar(out=gw_bf[:, cols, 3], in0=g_last[h][:], scalar1=rowf_t[:, 3:4], scalar2=None,
+                                    op0=ALU.mult)
+        for h in range(2):
+            cols = slice(h * half, (h + 1) * half)
+            nc.vector.quantize_mx(out=gw_w[:, cols].bitcast(FP8X4), scales=gw_sc[:, cols],
+                                  in_=gw_bf[:, cols, :].rearrange("p i r -> p (i r)"))
+            bank = psum.tile([P, 2, half], F32, name="y%d" % h)
+            for eh in range(2):
+                nc.tensor.matmul_mx(out=bank[:, eh, :], lhsT=mix_w[:, eh * P:(eh + 1) * P].bitcast(FP8X4),
+                                    lhsT_scale=mix_sc[:, eh * P:(eh + 1) * P], rhs=gw_w[:, cols].bitcast(FP8X4),
+                                    rhs_scale=gw_sc[:, cols], start=True, stop=True)
+            y = keep.tile([P, 2, half], F32, name="y_sb%d" % h)
+            if h == 0:
+                nc.scalar.copy(out=y[:], in_=bank[:])
+            else:
+                nc.vector.tensor_copy(out=y[:], in_=bank[:])
+            nc.sync.dma_start(out=out.rearrange("(eh p) i -> p eh i", p=P)[:, :, cols], in_=y[:])

@@ -26,7 +26,6 @@ def tile_attend_pairopen_threeq_mixed_kernel(tc, query, query2, keys_words, keys
     nc = tc.nc
     with ExitStack() as ctx:
         keep = ctx.enter_context(tc.tile_pool(name="keep", bufs=1))
-        ring = ctx.enter_context(tc.tile_pool(name="ring", bufs=2))
         psum = ctx.enter_context(tc.psum_pool(name="psum", bufs=1))
 
         def plane(name, width, engine):
@@ -42,8 +41,8 @@ def tile_attend_pairopen_threeq_mixed_kernel(tc, query, query2, keys_words, keys
         def load_words(t, src):
             nc.sync.dma_start(out=t[:].bitcast(I32), in_=src[0].rearrange("p n t -> p (n t)").bitcast(I32))
 
-        def load_query(name, src, h, tag=None):
-            t = keep.tile([P, PACK, Q // 2], F32, name="%s%d" % (name, h), tag=tag or "%s%d" % (name, h), align_bytes=64)
+        def load_query(name, src, h):
+            t = keep.tile([P, PACK, Q // 2], F32, name="%s%d" % (name, h))
             nc.sync.dma_start(out=t[:], in_=src.rearrange("(p t) q -> p t q", t=PACK)[:, :, h * 256:(h + 1) * 256])
             return t
 
@@ -54,7 +53,7 @@ def tile_attend_pairopen_threeq_mixed_kernel(tc, query, query2, keys_words, keys
 
         def load_rows(name, src):
             t = keep.tile([P, PACK], F32, name=name)
-            nc.sync.dma_start(out=t[:], in_=src.rearrange("(p r) o -> p (r o)", r=PACK))
+            nc.gpsimd.dma_start(out=t[:], in_=src.rearrange("(p r) o -> p (r o)", r=PACK))
             return t
 
         keys_sc = plane("keys_sc", T, nc.gpsimd)
@@ -75,23 +74,22 @@ def tile_attend_pairopen_threeq_mixed_kernel(tc, query, query2, keys_words, keys
         nc.sync.dma_start(out=keys_w[:].bitcast(I32), in_=keys_words[0].bitcast(I32))
         load_words(notes_w, notes_words)
         list_a = load_list("list_a", offs, I)
+        load_plane(nc.sync, notes_sc, notes_scales)
+        list_b = load_list("list_b", offs2, I)
+        q2_raw = [load_query("q2_raw", query2, h) for h in range(2)]
+        list_p = load_list("list_p", offs3, J)
+        load_words(users_w, users_words)
+        list_g = load_list("list_g", offs4, I)
+        load_words(mix_w, mix_words)
         slope_t = load_rows("slope_t", slope)
         thr_t = load_rows("thr_t", thr)
-        load_plane(nc.sync, notes_sc, notes_scales)
-        q2_raw = [load_query("q2_raw", query2, 0)]
-        list_b = load_list("list_b", offs2, I)
-        q2_raw.append(load_query("q2_raw", query2, 1, "shared"))
-        load_plane(nc.sync, users_sc, users_scales)
-        load_words(users_w, users_words)
-        list_p = load_list("list_p", offs3, J)
-        list_g = load_list("list_g", offs4, I)
+        load_plane(nc.gpsimd, users_sc, users_scales)
         rowf_t = load_rows("rowf_t", rowf)
-        load_words(mix_w, mix_words)
-        load_plane(nc.sync, mix_sc, mix_scales)
+        load_plane(nc.gpsimd, mix_sc, mix_scales)
 
         def deal(copy, dealt, raw, h):
-            copy(out=dealt[:, :, 64 * h:64 * h + 64, :].rearrange("p r m t -> p m r t"),
-                 in_=raw[:].rearrange("p t (m r) -> p m r t", r=PACK))
+            copy(out=dealt[:, :, 64 * h:64 * h + 64, :].rearrange("p r m t -> p m t r"),
+                 in_=raw[:].rearrange("p t (m r) -> p m t r", r=PACK))
 
         def quantise(codes, scales, dealt, r0, r1):
             nc.vector.quantize_mx(out=codes[:, r0 * P:r1 * P].bitcast(FP8X4), scales=scales[:, r0 * P:r1 * P],
@@ -127,84 +125,117 @@ def tile_attend_pairopen_threeq_mixed_kernel(tc, query, query2, keys_words, keys
                 copy(out=t[:, h * BANK:(h + 1) * BANK], in_=banks[h][:])
             return t
 
-        def gate(a_sb, r):
-            s1 = ring.tile([P, I], F32, name="s1")
-            nc.scalar.activation(out=s1[:], in_=a_sb[:].indirect(list_a[:]), func=ACT.Sigmoid,
-                                 bias=thr_t[:, r:r + 1], scale=slope_t[:, r:r + 1])
-            return s1
+        def vector_gather(out_ap, window, offsets):
+            nc.vector.tensor_copy(out=out_ap, in_=window.indirect(offsets))
+
+        def scalar_gather(out_ap, window, offsets):
+            nc.scalar.activation(out=out_ap, in_=window.indirect(offsets), func=ACT.Copy)
+
+        picked = {}
+        b_sb = {}
+        w = {}
+        cc = {}
+        g = {}
 
         def front(r, copy):
             a_banks = scores("a", q1_w, q1_sc, keys_rhs, keys_sc, r)
             b_banks = scores("b", q1_w, q1_sc, notes_rhs, notes_sc, r)
-            a_sb = to_sbuf(keep.tile([P, T], F32, name="a_sb", tag="a_first" if r == 0 else "shared", align_bytes=64), a_banks, copy)
-            b_sb = to_sbuf(ring.tile([P, T], F32, name="b_sb"), b_banks, copy)
-            return gate(a_sb, r), b_sb
+            a_sb = to_sbuf(keep.tile([P, T], F32, name="a_sb"), a_banks, copy)
+            b_sb[r] = to_sbuf(keep.tile([P, T], F32, name="b_sb%d" % r), b_banks, copy)
+            picked[r] = keep.tile([P, 2, I], F32, name="picked%d" % r)
+            nc.scalar.activation(out=picked[r][:, 0, :], in_=a_sb[:].indirect(list_a[:]), func=ACT.Sigmoid,
+                                 bias=thr_t[:, r:r + 1], scale=slope_t[:, r:r + 1])
 
-        def pairs(s1, b_sb):
-            w = ring.tile([P, I], F32, name="w")
-            nc.vector.tensor_tensor(out=w[:], in0=b_sb[:].indirect(list_b[:]), in1=s1[:], op=ALU.mult)
-            p2 = ring.tile([P, J], F32, name="p2")
-            nc.vector.tensor_tensor(out=p2[:], in0=w[:, 0:I:2], in1=w[:, 1:I:2], op=ALU.add)
-            nc.vector.tensor_copy(out=f1[:].indirect(list_p[:]), in_=p2[:])
+        def pick_b(r, gather):
+            gather(picked[r][:, 1, :], b_sb[r][:], list_b[:])
+
+        def gated(r):
+            w[r] = keep.tile([P, 2, J], F32, name="w%d" % r)
+            nc.vector.tensor_tensor(out=w[r][:], in0=picked[r][:, 1, :].rearrange("p (j s) -> p s j", s=2),
+                                    in1=picked[r][:, 0, :].rearrange("p (j s) -> p s j", s=2), op=ALU.mult)
+
+        def put(r):
+            nc.vector.tensor_tensor(out=f1[:].indirect(list_p[:]), in0=w[r][:, 0, :], in1=w[r][:, 1, :], op=ALU.add)
 
         def users_sum(r):
             c_banks = scores("c", q2_w, q2_sc, users_rhs, users_sc, r)
-            cc = keep.tile([P, T], F32, name="cc%d" % r)
+            cc[r] = keep.tile([P, T], F32, name="cc%d" % r, tag="picked3" if r == 2 else "cc%d" % r)
             for h in range(2):
                 cols = slice(h * BANK, (h + 1) * BANK)
-                nc.vector.tensor_tensor(out=cc[:, cols], in0=c_banks[h][:], in1=f1[:, cols], op=ALU.add)
-            return cc
+                nc.vector.tensor_tensor(out=cc[r][:, cols], in0=c_banks[h][:], in1=f1[:, cols], op=ALU.add)
+
+        def pick_g(r):
+            g[r] = keep.tile([P, I], F32, name="g%d" % r)
+            scalar_gather(g[r][:], cc[r][:], list_g[:])
+
+        def factor(r):
+            nc.vector.tensor_scalar(out=gw3[:, r, :], in0=g[r][:], scalar1=rowf_t[:, r:r + 1], scalar2=None,
+                                    op0=ALU.mult)
 
         gw3 = keep.tile([P, PACK - 1, I], F32, name="gw3")
         gw_bf = keep.tile([P, I, PACK], BF16, name="gw_bf", align_bytes=64)
 
-        deal(nc.scalar.copy, q1_bf, q1_raw[0], 0)
+        deal(nc.vector.tensor_copy, q1_bf, q1_raw[0], 0)
         deal(nc.vector.tensor_copy, q1_bf, q1_raw[1], 1)
         quantise(q1_w, q1_sc, q1_bf, 0, 1)
         quantise(q1_w, q1_sc, q1_bf, 1, 4)
+        q2_bf = keep.tile([P, PACK, P, PACK], BF16, name="q2_bf", align_bytes=64)
 
-        ready = front(0, nc.vector.tensor_copy)
-        q2_bf = keep.tile([P, PACK, P, PACK], BF16, name="q2_bf", tag="a_first", align_bytes=64)
-        deal(nc.scalar.copy, q2_bf, q2_raw[0], 0)
-        deal(nc.scalar.copy, q2_bf, q2_raw[1], 1)
-        sums = []
-        for r in range(PACK):
-            s1, b_sb = ready
-            if r + 1 < PACK:
-                ready = front(r + 1, nc.scalar.copy)
-            pairs(s1, b_sb)
-            if r == 0:
-                quantise(q2_w, q2_sc, q2_bf, 0, 4)
-            sums.append(users_sum(r))
-        for r in range(PACK - 1):
-            g = ring.tile([P, I], F32, name="g")
-            nc.scalar.activation(out=g[:], in_=sums[r][:].indirect(list_g[:]), func=ACT.Copy)
-            nc.scalar.activation(out=gw3[:, r, :], in_=g[:], func=ACT.Copy, scale=rowf_t[:, r:r + 1])
-        nc.vector.tensor_copy(out=gw_bf[:, :, 0:3], in_=gw3[:].rearrange("p r i -> p i r"))
-        cc = sums[PACK - 1]
+        front(0, nc.vector.tensor_copy)
+        for r in range(1, PACK):
+            front(r, nc.scalar.copy)
+        pick_b(3, scalar_gather)
+
+        pick_b(0, vector_gather)
+        deal(nc.vector.tensor_copy, q2_bf, q2_raw[0], 0)
+        gated(0)
+        deal(nc.vector.tensor_copy, q2_bf, q2_raw[1], 1)
+        put(0)
+        quantise(q2_w, q2_sc, q2_bf, 0, 4)
+        pick_b(1, vector_gather)
+        users_sum(0)
+        gated(1)
+        pick_b(2, vector_gather)
+        put(1)
+        gated(2)
+        users_sum(1)
+        put(2)
+        gated(3)
+        users_sum(2)
+        pick_g(0)
+        factor(0)
+        put(3)
+        pick_g(1)
+        factor(1)
+        users_sum(3)
+        pick_g(2)
+        factor(2)
+        nc.vector.tensor_copy(out=gw_bf[:, :, 0:3].rearrange("p (c i) r -> p c r i", i=4),
+                              in_=gw3[:].rearrange("p r (c i) -> p c r i", i=4))
 
         half = I // 2
         g_last = [keep.tile([P, half], F32, name="g_last%d" % h) for h in range(2)]
-        nc.vector.tensor_copy(out=g_last[0][:], in_=cc[:].indirect(list_g[:, 0:16]))
-        nc.scalar.activation(out=g_last[1][:], in_=cc[:].indirect(list_g[:, 16:32]), func=ACT.Copy)
+        for h in range(2):
+            scalar_gather(g_last[h][:], cc[3][:], list_g[:, 16 * h:16 * h + 16])
         gw_w = keep.tile([P, I], U32, name="gw_w", align_bytes=64)
         gw_sc = keep.tile([P, I], U8, name="gw_sc", align_bytes=64)
         for h in range(2):
             cols = slice(h * half, (h + 1) * half)
             nc.vector.tensor_scalar(out=gw_bf[:, cols, 3], in0=g_last[h][:], scalar1=rowf_t[:, 3:4], scalar2=None,
                                     op0=ALU.mult)
-        for h in range(2):
-            cols = slice(h * half, (h + 1) * half)
             nc.vector.quantize_mx(out=gw_w[:, cols].bitcast(FP8X4), scales=gw_sc[:, cols],
                                   in_=gw_bf[:, cols, :].rearrange("p i r -> p (i r)"))
-            bank = psum.tile([P, 2, half], F32, name="y%d" % h)
+        for h in range(2):
+            cols = slice(h * half, (h + 1) * half)
             for eh in range(2):
-                nc.tensor.matmul_mx(out=bank[:, eh, :], lhsT=mix_w[:, eh * P:(eh + 1) * P].bitcast(FP8X4),
+                bank = psum.tile([P, BANK], F32, name="y", tag="ab"[h] + str(eh))
+                nc.tensor.matmul_mx(out=bank[:, 0:half], lhsT=mix_w[:, eh * P:(eh + 1) * P].bitcast(FP8X4),
                                     lhsT_scale=mix_sc[:, eh * P:(eh + 1) * P], rhs=gw_w[:, cols].bitcast(FP8X4),
                                     rhs_scale=gw_sc[:, cols], start=True, stop=True)
-            y = keep.tile([P, 2, half], F32, name="y_sb%d" % h)
-            if h == 0:
-                nc.scalar.copy(out=y[:], in_=bank[:])
-            else:
-                nc.vector.tensor_copy(out=y[:], in_=bank[:])
-            nc.sync.dma_start(out=out.rearrange("(eh p) i -> p eh i", p=P)[:, :, cols], in_=y[:])
+                y = keep.tile([P, half], F32, name="y_sb%d%d" % (h, eh))
+                if h == 1 and eh == 1:
+                    nc.vector.tensor_copy(out=y[:], in_=bank[:, 0:half])
+                    nc.sync.dma_start(out=out[eh * P:(eh + 1) * P, cols], in_=y[:])
+                else:
+                    nc.scalar.copy(out=y[:], in_=bank[:, 0:half])
+                    (nc.scalar if h == 1 else nc.sync).dma_start(out=out[eh * P:(eh + 1) * P, cols], in_=y[:])

@@ -81,11 +81,11 @@ def tile_attend_pairopen_threeq_mixed_kernel(tc, query, query2, keys_words, keys
         load_words(users_w, users_words)
         list_g = load_list("list_g", offs4, I)
         load_words(mix_w, mix_words)
+        load_plane(nc.sync, mix_sc, mix_scales)
         slope_t = load_rows("slope_t", slope)
         thr_t = load_rows("thr_t", thr)
         load_plane(nc.gpsimd, users_sc, users_scales)
         rowf_t = load_rows("rowf_t", rowf)
-        load_plane(nc.gpsimd, mix_sc, mix_scales)
 
         def deal(copy, dealt, raw, h):
             copy(out=dealt[:, :, 64 * h:64 * h + 64, :].rearrange("p r m t -> p m t r"),
@@ -150,25 +150,30 @@ def tile_attend_pairopen_threeq_mixed_kernel(tc, query, query2, keys_words, keys
             gather(picked[r][:, 1, :], b_sb[r][:], list_b[:])
 
         def gated(r):
-            w[r] = keep.tile([P, 2, J], F32, name="w%d" % r)
-            nc.vector.tensor_tensor(out=w[r][:], in0=picked[r][:, 1, :].rearrange("p (j s) -> p s j", s=2),
+            w[r] = keep.tile([P, 2, J], F32, name="w")
+            (nc.vector if r == 0 else nc.gpsimd).tensor_tensor(out=w[r][:], in0=picked[r][:, 1, :].rearrange("p (j s) -> p s j", s=2),
                                     in1=picked[r][:, 0, :].rearrange("p (j s) -> p s j", s=2), op=ALU.mult)
 
         def put(r):
             nc.vector.tensor_tensor(out=f1[:].indirect(list_p[:]), in0=w[r][:, 0, :], in1=w[r][:, 1, :], op=ALU.add)
 
-        def users_sum(r):
-            c_banks = scores("c", q2_w, q2_sc, users_rhs, users_sc, r)
-            cc[r] = keep.tile([P, T], F32, name="cc%d" % r, tag="picked3" if r == 2 else "cc%d" % r)
-            for h in range(2):
-                cols = slice(h * BANK, (h + 1) * BANK)
-                nc.vector.tensor_tensor(out=cc[r][:, cols], in0=c_banks[h][:], in1=f1[:, cols], op=ALU.add)
+        c_banks = {}
+
+        def users_sum(r, h):
+            if h == 0:
+                c_banks[r] = scores("c", q2_w, q2_sc, users_rhs, users_sc, r)
+                cc[r] = keep.tile([P, T], F32, name="cc%d" % r, tag="cc%d" % r)
+            cols = slice(h * BANK, (h + 1) * BANK)
+            nc.vector.tensor_tensor(out=cc[r][:, cols], in0=c_banks[r][h][:], in1=f1[:, cols], op=ALU.add)
 
         def pick_g(r):
-            g[r] = keep.tile([P, I], F32, name="g%d" % r)
+            g[r] = keep.tile([P, I], F32, name="g%d" % r, tag=("a_sb", "b_sb3", "g2")[r])
             scalar_gather(g[r][:], cc[r][:], list_g[:])
 
         def factor(r):
+            nc.scalar.activation(out=gw3[:, r, :], in_=g[r][:], func=ACT.Copy, scale=rowf_t[:, r:r + 1])
+
+        def vector_factor(r):
             nc.vector.tensor_scalar(out=gw3[:, r, :], in0=g[r][:], scalar1=rowf_t[:, r:r + 1], scalar2=None,
                                     op0=ALU.mult)
 
@@ -193,23 +198,27 @@ def tile_attend_pairopen_threeq_mixed_kernel(tc, query, query2, keys_words, keys
         put(0)
         quantise(q2_w, q2_sc, q2_bf, 0, 4)
         pick_b(1, vector_gather)
-        users_sum(0)
         gated(1)
-        pick_b(2, vector_gather)
+        users_sum(0, 0)
+        users_sum(0, 1)
         put(1)
+        pick_b(2, vector_gather)
         gated(2)
-        users_sum(1)
+        users_sum(1, 0)
+        users_sum(1, 1)
         put(2)
         gated(3)
-        users_sum(2)
-        pick_g(0)
-        factor(0)
+        users_sum(2, 0)
+        users_sum(2, 1)
         put(3)
+        pick_g(0)
+        vector_factor(0)
+        users_sum(3, 0)
+        users_sum(3, 1)
         pick_g(1)
         factor(1)
-        users_sum(3)
         pick_g(2)
-        factor(2)
+        vector_factor(2)
         nc.vector.tensor_copy(out=gw_bf[:, :, 0:3].rearrange("p (c i) r -> p c r i", i=4),
                               in_=gw3[:].rearrange("p r (c i) -> p c r i", i=4))
 

from contextlib import ExitStack

import concourse.mybir as mybir

F32 = mybir.dt.float32
BF16 = mybir.dt.bfloat16
I32 = mybir.dt.int32
U32 = mybir.dt.uint32
U16 = mybir.dt.uint16
U8 = mybir.dt.uint8
FP8X4 = mybir.dt.float8_e4m3fn_x4
FP4X4 = mybir.dt.float4_e2m1fn_x4
ACT = mybir.ActivationFunctionType
ALU = mybir.AluOpType

P = 128
PACK = 4
D, T, I, J, Q, E = 512, 1024, 512, 256, 512, 256
BANK = 512
FLOPS = 2 * D * Q * 3 * T + 2 * Q * E * I


def tile_attend_pairopen_threeq_mixed_kernel(tc, query, query2, keys_words, keys_scales, notes_words, notes_scales,
                                              users_words, users_scales, thr, slope, rowf, mix_words, mix_scales,
                                              offs, offs2, offs3, offs4, out):
    nc = tc.nc
    with ExitStack() as ctx:
        keep = ctx.enter_context(tc.tile_pool(name="keep", bufs=1))
        psum = ctx.enter_context(tc.psum_pool(name="psum", bufs=1))

        def plane(name, width, engine):
            t = keep.tile([P, width], U8, name=name, align_bytes=64)
            engine.memset(t[:].bitcast(I32), 0)
            return t

        def load_plane(queue, t, src):
            for quad in range(4):
                queue.dma_start(out=t[32 * quad:32 * quad + 4, :].bitcast(I32),
                                in_=src[0, 4 * quad:4 * quad + 4, :].bitcast(I32))

        def load_words(t, src):
            nc.sync.dma_start(out=t[:].bitcast(I32), in_=src[0].rearrange("p n t -> p (n t)").bitcast(I32))

        def load_query(name, src, h):
            t = keep.tile([P, PACK, Q // 2], F32, name="%s%d" % (name, h))
            nc.sync.dma_start(out=t[:], in_=src.rearrange("(p t) q -> p t q", t=PACK)[:, :, h * 256:(h + 1) * 256])
            return t

        def load_list(name, src, n):
            t = keep.tile([P, n // 16], U16, name=name)
            nc.sync.dma_start(t[:], src)
            return t

        def load_rows(name, src):
            t = keep.tile([P, PACK], F32, name=name)
            nc.gpsimd.dma_start(out=t[:], in_=src.rearrange("(p r) o -> p (r o)", r=PACK))
            return t

        keys_sc = plane("keys_sc", T, nc.gpsimd)
        notes_sc = plane("notes_sc", T, nc.gpsimd)
        users_sc = plane("users_sc", T, nc.vector)
        mix_sc = plane("mix_sc", E, nc.vector)
        f1 = keep.tile([P, T], F32, name="f1")
        nc.vector.memset(f1[:], 0.0)

        keys_w = keep.tile([P, 2 * T], U8, name="keys_w", align_bytes=64)
        notes_w = keep.tile([P, T], U32, name="notes_w", align_bytes=64)
        users_w = keep.tile([P, T], U32, name="users_w", align_bytes=64)
        mix_w = keep.tile([P, E], U32, name="mix_w", align_bytes=64)

        q1_raw = [load_query("q1_raw", query, 0)]
        load_plane(nc.sync, keys_sc, keys_scales)
        q1_raw.append(load_query("q1_raw", query, 1))
        nc.sync.dma_start(out=keys_w[:].bitcast(I32), in_=keys_words[0].bitcast(I32))
        load_words(notes_w, notes_words)
        list_a = load_list("list_a", offs, I)
        load_plane(nc.sync, notes_sc, notes_scales)
        list_b = load_list("list_b", offs2, I)
        q2_raw = [load_query("q2_raw", query2, h) for h in range(2)]
        list_p = load_list("list_p", offs3, J)
        load_words(users_w, users_words)
        list_g = load_list("list_g", offs4, I)
        load_words(mix_w, mix_words)
        load_plane(nc.sync, mix_sc, mix_scales)
        slope_t = load_rows("slope_t", slope)
        thr_t = load_rows("thr_t", thr)
        load_plane(nc.gpsimd, users_sc, users_scales)
        rowf_t = load_rows("rowf_t", rowf)

        def deal(copy, dealt, raw, h):
            copy(out=dealt[:, :, 64 * h:64 * h + 64, :].rearrange("p r m t -> p m t r"),
                 in_=raw[:].rearrange("p t (m r) -> p m t r", r=PACK))

        def quantise(codes, scales, dealt, r0, r1):
            nc.vector.quantize_mx(out=codes[:, r0 * P:r1 * P].bitcast(FP8X4), scales=scales[:, r0 * P:r1 * P],
                                  in_=dealt[:, r0:r1, :, :].rearrange("p r m t -> p (r m t)"))

        q1_bf = keep.tile([P, PACK, P, PACK], BF16, name="q1_bf", align_bytes=64)
        q1_w = keep.tile([P, Q], U32, name="q1_w", align_bytes=64)
        q2_w = keep.tile([P, Q], U32, name="q2_w", align_bytes=64)
        q1_sc = keep.tile([P, Q], U8, name="q1_sc", align_bytes=64)
        q2_sc = keep.tile([P, Q], U8, name="q2_sc", align_bytes=64)

        def scores(tag, q_w, q_sc, rhs_of, rhs_sc, r):
            banks = []
            for h in range(2):
                bank = psum.tile([P, BANK], F32, name="%s%d" % (tag, h))
                nc.tensor.matmul_mx(out=bank[:], lhsT=q_w[:, r * P:(r + 1) * P].bitcast(FP8X4),
                                    lhsT_scale=q_sc[:, r * P:(r + 1) * P], rhs=rhs_of(h),
                                    rhs_scale=rhs_sc[:, h * BANK:(h + 1) * BANK], start=True, stop=True)
                banks.append(bank)
            return banks

        def keys_rhs(h):
            return keys_w[:, 2 * h * BANK:2 * (h + 1) * BANK].bitcast(FP4X4)

        def notes_rhs(h):
            return notes_w[:, h * BANK:(h + 1) * BANK].bitcast(FP8X4)

        def users_rhs(h):
            return users_w[:, h * BANK:(h + 1) * BANK].bitcast(FP8X4)

        def to_sbuf(t, banks, copy):
            for h in range(2):
                copy(out=t[:, h * BANK:(h + 1) * BANK], in_=banks[h][:])
            return t

        def vector_gather(out_ap, window, offsets):
            nc.vector.tensor_copy(out=out_ap, in_=window.indirect(offsets))

        def scalar_gather(out_ap, window, offsets):
            nc.scalar.activation(out=out_ap, in_=window.indirect(offsets), func=ACT.Copy)

        picked = {}
        b_sb = {}
        w = {}
        cc = {}
        g = {}

        def front(r, copy):
            a_banks = scores("a", q1_w, q1_sc, keys_rhs, keys_sc, r)
            b_banks = scores("b", q1_w, q1_sc, notes_rhs, notes_sc, r)
            a_sb = to_sbuf(keep.tile([P, T], F32, name="a_sb"), a_banks, copy)
            b_sb[r] = to_sbuf(keep.tile([P, T], F32, name="b_sb%d" % r), b_banks, copy)
            picked[r] = keep.tile([P, 2, I], F32, name="picked%d" % r)
            nc.scalar.activation(out=picked[r][:, 0, :], in_=a_sb[:].indirect(list_a[:]), func=ACT.Sigmoid,
                                 bias=thr_t[:, r:r + 1], scale=slope_t[:, r:r + 1])

        def pick_b(r, gather):
            gather(picked[r][:, 1, :], b_sb[r][:], list_b[:])

        def gated(r):
            w[r] = keep.tile([P, 2, J], F32, name="w")
            (nc.vector if r == 0 else nc.gpsimd).tensor_tensor(out=w[r][:], in0=picked[r][:, 1, :].rearrange("p (j s) -> p s j", s=2),
                                    in1=picked[r][:, 0, :].rearrange("p (j s) -> p s j", s=2), op=ALU.mult)

        def put(r):
            nc.vector.tensor_tensor(out=f1[:].indirect(list_p[:]), in0=w[r][:, 0, :], in1=w[r][:, 1, :], op=ALU.add)

        c_banks = {}

        def users_sum(r, h):
            if h == 0:
                c_banks[r] = scores("c", q2_w, q2_sc, users_rhs, users_sc, r)
                cc[r] = keep.tile([P, T], F32, name="cc%d" % r, tag="cc%d" % r)
            cols = slice(h * BANK, (h + 1) * BANK)
            nc.vector.tensor_tensor(out=cc[r][:, cols], in0=c_banks[r][h][:], in1=f1[:, cols], op=ALU.add)

        def pick_g(r):
            g[r] = keep.tile([P, I], F32, name="g%d" % r, tag=("a_sb", "b_sb3", "g2")[r])
            scalar_gather(g[r][:], cc[r][:], list_g[:])

        def factor(r):
            nc.scalar.activation(out=gw3[:, r, :], in_=g[r][:], func=ACT.Copy, scale=rowf_t[:, r:r + 1])

        def vector_factor(r):
            nc.vector.tensor_scalar(out=gw3[:, r, :], in0=g[r][:], scalar1=rowf_t[:, r:r + 1], scalar2=None,
                                    op0=ALU.mult)

        gw3 = keep.tile([P, PACK - 1, I], F32, name="gw3")
        gw_bf = keep.tile([P, I, PACK], BF16, name="gw_bf", align_bytes=64)

        deal(nc.vector.tensor_copy, q1_bf, q1_raw[0], 0)
        deal(nc.vector.tensor_copy, q1_bf, q1_raw[1], 1)
        quantise(q1_w, q1_sc, q1_bf, 0, 1)
        quantise(q1_w, q1_sc, q1_bf, 1, 4)
        q2_bf = keep.tile([P, PACK, P, PACK], BF16, name="q2_bf", align_bytes=64)

        front(0, nc.vector.tensor_copy)
        for r in range(1, PACK):
            front(r, nc.scalar.copy)
        pick_b(3, scalar_gather)

        pick_b(0, vector_gather)
        deal(nc.vector.tensor_copy, q2_bf, q2_raw[0], 0)
        gated(0)
        deal(nc.vector.tensor_copy, q2_bf, q2_raw[1], 1)
        put(0)
        quantise(q2_w, q2_sc, q2_bf, 0, 4)
        pick_b(1, vector_gather)
        gated(1)
        users_sum(0, 0)
        users_sum(0, 1)
        put(1)
        pick_b(2, vector_gather)
        gated(2)
        users_sum(1, 0)
        users_sum(1, 1)
        put(2)
        gated(3)
        users_sum(2, 0)
        users_sum(2, 1)
        put(3)
        pick_g(0)
        vector_factor(0)
        users_sum(3, 0)
        users_sum(3, 1)
        pick_g(1)
        factor(1)
        pick_g(2)
        vector_factor(2)
        nc.vector.tensor_copy(out=gw_bf[:, :, 0:3].rearrange("p (c i) r -> p c r i", i=4),
                              in_=gw3[:].rearrange("p r (c i) -> p c r i", i=4))

        half = I // 2
        g_last = [keep.tile([P, half], F32, name="g_last%d" % h) for h in range(2)]
        for h in range(2):
            scalar_gather(g_last[h][:], cc[3][:], list_g[:, 16 * h:16 * h + 16])
        gw_w = keep.tile([P, I], U32, name="gw_w", align_bytes=64)
        gw_sc = keep.tile([P, I], U8, name="gw_sc", align_bytes=64)
        for h in range(2):
            cols = slice(h * half, (h + 1) * half)
            nc.vector.tensor_scalar(out=gw_bf[:, cols, 3], in0=g_last[h][:], scalar1=rowf_t[:, 3:4], scalar2=None,
                                    op0=ALU.mult)
            nc.vector.quantize_mx(out=gw_w[:, cols].bitcast(FP8X4), scales=gw_sc[:, cols],
                                  in_=gw_bf[:, cols, :].rearrange("p i r -> p (i r)"))
        for h in range(2):
            cols = slice(h * half, (h + 1) * half)
            for eh in range(2):
                bank = psum.tile([P, BANK], F32, name="y", tag="ab"[h] + str(eh))
                nc.tensor.matmul_mx(out=bank[:, 0:half], lhsT=mix_w[:, eh * P:(eh + 1) * P].bitcast(FP8X4),
                                    lhsT_scale=mix_sc[:, eh * P:(eh + 1) * P], rhs=gw_w[:, cols].bitcast(FP8X4),
                                    rhs_scale=gw_sc[:, cols], start=True, stop=True)
                y = keep.tile([P, half], F32, name="y_sb%d%d" % (h, eh))
                if h == 1 and eh == 1:
                    nc.vector.tensor_copy(out=y[:], in_=bank[:, 0:half])
                    nc.sync.dma_start(out=out[eh * P:(eh + 1) * P, cols], in_=y[:])
                else:
                    nc.scalar.copy(out=y[:], in_=bank[:, 0:half])
                    (nc.scalar if h == 1 else nc.sync).dma_start(out=out[eh * P:(eh + 1) * P, cols], in_=y[:])
